import numpy as np
import ml_dtypes


def mxq(x, axis, fmt="e4m3"):
    dtype, down = {"e4m3": (ml_dtypes.float8_e4m3fn, 7), "e5m2": (ml_dtypes.float8_e5m2, 14)}[fmt]
    v = np.moveaxis(np.asarray(x, np.float32).astype(ml_dtypes.bfloat16).astype(np.float64), axis, -1)
    blocks = v.reshape(v.shape[:-1] + (-1, 32))
    amax = np.abs(blocks).max(-1, keepdims=True)
    byte = np.maximum(np.where(amax > 0, np.frexp(amax)[1] - 1 + 127, 0) - down, 1)
    scale = np.exp2(byte - 127.0)
    codes = (blocks / scale).astype(np.float32).astype(dtype).astype(np.float64)
    return np.moveaxis((codes * scale).reshape(v.shape), -1, axis)


WIDE = False


def mx_kscale(k):
    if not WIDE:
        return np.ones(k)
    levels = np.array([10, -10, 5, -5, 0])
    if k % 512:
        return np.exp2(np.random.permutation(np.resize(levels, k // 32))).repeat(32)
    a = np.empty((k // 512, 16))
    for p in range(k // 512):
        a[p, :8] = np.random.permutation(np.resize(levels, 8))
        for g in range(8):
            far = levels[np.abs(levels - a[p, g]) >= 10]
            a[p, g + 8] = far[np.random.randint(len(far))]
    return np.exp2(a.ravel()).repeat(32)


def f64(x):
    return np.asarray(x).astype(np.float64)


def striped(idx):
    return np.tile(idx.reshape(-1, 16).T, (8, 1)).astype(np.uint16)


def unstriped(offs):
    return offs[:16].T.reshape(-1).astype(np.int64)


def striped8(idx):
    return np.concatenate([x.reshape(-1, 16).T for x in idx]).astype(np.uint16)


def runs(offs, k):
    lists = np.stack([offs[16 * r : 16 * r + 16].T.reshape(-1) for r in range(8)]).astype(np.int64)
    return lists[np.arange(k) % 512 // 64]


def pack_weight(w):
    k, n = w.shape
    w = f64(np.asarray(w, np.float32).astype(ml_dtypes.bfloat16)).reshape(k // 32, 32, n)
    amax = np.abs(w).max(1)
    byte = np.clip(np.where(amax > 0, np.frexp(amax)[1] - 1 + 127 - 7, 1), 1, 254)
    scaled = (w * np.exp2(127.0 - byte)[:, None, :]).reshape(k, n).astype(np.float32)
    words = np.ascontiguousarray(scaled.reshape(k // 512, 128, 4, n).transpose(0, 1, 3, 2)).astype(ml_dtypes.float8_e4m3fn).view(np.uint8)
    return words, np.ascontiguousarray(byte.astype(np.uint8).reshape(k // 512, 16, n))


def unpack_weight(words, scales):
    g, p, n, _ = words.shape
    vals = np.ascontiguousarray(words).view(ml_dtypes.float8_e4m3fn).astype(np.float64) * np.repeat(np.exp2(scales.astype(np.float64) - 127.0), 8, axis=1)[..., None]
    return vals.transpose(0, 1, 3, 2).reshape(g * 512, n)


E2M1 = np.array([0.0, 0.5, 1.0, 1.5, 2.0, 3.0, 4.0, 6.0, -0.0, -0.5, -1.0, -1.5, -2.0, -3.0, -4.0, -6.0])


def pack_fp4(w):
    k, n = w.shape
    w = f64(np.asarray(w, np.float32).astype(ml_dtypes.bfloat16)).reshape(k // 32, 32, n)
    amax = np.abs(w).max(1)
    mant, ex = np.frexp(amax / 6.0)
    byte = np.clip(np.where(amax > 0, np.where(mant > 0.5, ex, ex - 1) + 127, 1), 1, 254)
    scaled = (w * np.exp2(127.0 - byte)[:, None, :]).reshape(k, n).astype(np.float32)
    c = np.ascontiguousarray(scaled.reshape(k // 512, 128, 4, n).transpose(0, 1, 3, 2)).astype(ml_dtypes.float4_e2m1fn).view(np.uint8) & 0xF
    words = (c[..., 0::2] | (c[..., 1::2] << 4)).reshape(k // 512, 128, 2 * n)
    return np.ascontiguousarray(words), np.ascontiguousarray(byte.astype(np.uint8).reshape(k // 512, 16, n))


def unpack_fp4(words, scales):
    g, _, n = scales.shape
    words = np.ascontiguousarray(words).reshape(g, 128, n, 2)
    nib = np.empty((g, 128, n, 4), np.uint8)
    nib[..., 0::2] = words & 0xF
    nib[..., 1::2] = words >> 4
    vals = E2M1[nib] * np.repeat(np.exp2(scales.astype(np.float64) - 127.0), 8, axis=1)[..., None]
    return vals.transpose(0, 1, 3, 2).reshape(g * 512, n)


def sigmoid(v):
    return 1.0 / (1.0 + np.exp(-np.maximum(v, -700.0)))

def planes(y):
    n, m = y.shape
    v = y.astype(np.float32).astype(ml_dtypes.bfloat16).astype(np.float64).reshape(n // 32, 32, m)
    top = np.abs(v).max(1)
    byte = np.clip(np.where(top > 0, np.frexp(top)[1] - 1 + 127 - 7, 1), 1, 254)
    codes = (v * np.exp2(127.0 - byte)[:, None, :]).reshape(n, m).astype(np.float32).astype(ml_dtypes.float8_e4m3fn).view(np.uint8)
    words = codes.reshape(n // 512, 128, 4, m).transpose(0, 1, 3, 2)
    return np.ascontiguousarray(words), np.ascontiguousarray(byte.astype(np.uint8).reshape(n // 512, 16, m))


K, T, S, N, H, W = 512, 2048, 512, 512, 512, 256


def setup_inputs():
    n = np.random.standard_normal
    s = mx_kscale(K)[:, None]
    u = mx_kscale(H)
    packed_xT = pack_weight(n((K, T)) * s)
    packed_w1 = pack_fp4(n((K, H)) / np.sqrt(K) / s)
    packed_w2 = pack_fp4(n((H, N)) / np.sqrt(2 * H) / u[:, None])
    packed_w3 = pack_fp4(n((H, N)) / np.sqrt(2 * H) / u[:, None])
    perm = np.stack([np.random.permutation(S) for _ in range(8)])
    return {
        "x_words": packed_xT[0],
        "x_scales": packed_xT[1],
        "w1_words": packed_w1[0],
        "w1_scales": packed_w1[1],
        "gn": (np.random.uniform(0.5, 1.5, (H, 1)) * u[:, None]).astype(np.float32),
        "gm": (np.random.uniform(0.5, 1.5, (H, 1)) * u[:, None]).astype(np.float32),
        "w2_words": packed_w2[0],
        "w2_scales": packed_w2[1],
        "w3_words": packed_w3[0],
        "w3_scales": packed_w3[1],
        "offs": striped(np.random.permutation(T)[:S]),
        "n1": striped8(perm[:, :W]),
        "n2": striped8(perm[:, W:]),
        "n3": striped8(np.stack([np.random.permutation(S) for _ in range(8)])),
        "n4": striped8(np.stack([np.random.permutation(S) for _ in range(8)])),
        "n5": striped8(np.stack([np.random.permutation(S) for _ in range(8)])),
        "n6": striped8(np.stack([np.random.permutation(S) for _ in range(8)])),
    }


def reference(x_words, x_scales, w1_words, w1_scales, gn, gm, w2_words, w2_scales, w3_words, w3_scales, offs, n1, n2, n3, n4, n5, n6):
    xq = unpack_weight(x_words, x_scales)[:, unstriped(offs)]
    y = unpack_fp4(w1_words, w1_scales).T @ xq
    pa = y[np.arange(H)[:, None], runs(n1, H)]
    pb = y[np.arange(H)[:, None], runs(n2, H)]
    rb = pa - pb
    ra = 0.75 * (pa + pb)
    ds = np.zeros((H, S))
    ds[np.arange(H)[:, None], runs(n1, H)] = ra
    dt = ds.copy()
    dt[np.arange(H)[:, None], runs(n2, H)] = rb
    z = f64(gn) * dt
    st = y[np.arange(H)[:, None], runs(n3, H)] - y
    z2 = f64(gm) * (y * (sigmoid(st[np.arange(H)[:, None], runs(n4, H)])))
    h = unpack_fp4(w2_words, w2_scales).T @ mxq(z, 0, "e4m3") + unpack_fp4(w3_words, w3_scales).T @ mxq(z2, 0, "e4m3")
    out_0 = h * (sigmoid(h[np.arange(N)[:, None], runs(n5, N)] - (h[np.arange(N)[:, None], runs(n6, N)])))
    return (out_0,) + planes(out_0)

@@ -1,0 +1,202 @@
+from contextlib import ExitStack
+
+import concourse.mybir as mybir
+
+K, T, S, H, N, W = 512, 2048, 512, 512, 512, 256
+FLOPS = 2 * K * H * S + 2 * 2 * H * N * S
+
+F32 = mybir.dt.float32
+BF16 = mybir.dt.bfloat16
+I32 = mybir.dt.int32
+U32 = mybir.dt.uint32
+U16 = mybir.dt.uint16
+U8 = mybir.dt.uint8
+FP8X4 = mybir.dt.float8_e4m3fn_x4
+FP4X4 = mybir.dt.float4_e2m1fn_x4
+ALU = mybir.AluOpType
+ACT = mybir.ActivationFunctionType
+
+P = 128
+PACK = 4
+QUADRANTS = 4
+LANES = 16
+CHUNKS = ((0, 256), (256, 384), (384, 512))
+
+
+def load_scale_rows(queues, plane, rows):
+    for q in range(QUADRANTS):
+        queues[q].dma_start(out=plane[32 * q : 32 * q + 4, :].bitcast(I32), in_=rows[0, 4 * q : 4 * q + 4, :].bitcast(I32))
+
+
+def tile_picked_joinhaarhopdcmp_none_po_kernel(
+    tc, x_words, x_scales, w1_words, w1_scales, gn, gm, w2_words, w2_scales, w3_words, w3_scales,
+    offs, n1, n2, n3, n4, n5, n6, out_0, out_1, out_2,
+):
+    nc = tc.nc
+    with ExitStack() as ctx:
+        sb = ctx.enter_context(tc.tile_pool(name="sb", bufs=1))
+        ps = ctx.enter_context(tc.psum_pool(name="ps", bufs=1))
+
+        def tile(shape, dtype, name):
+            return sb.tile(shape, dtype, name=name, align_bytes=64)
+
+        def tiles(shape, dtype, name):
+            return [tile(shape, dtype, "%s%d" % (name, t)) for t in range(PACK)]
+
+        def load_list(src, name):
+            lst = tile(list(src.shape), U16, name)
+            nc.sync.dma_start(lst[:], src)
+            return lst
+
+        x_scale_tab = tile([P, T], U8, "x_scale_tab")
+        w_scale_raw = [tile([P, H], U8, "w_scale_raw%d" % i) for i in range(3)]
+        nc.vector.memset(x_scale_tab[:].bitcast(I32), 0)
+        for i in range(3):
+            nc.vector.memset(w_scale_raw[i][:].bitcast(I32), 0)
+        load_scale_rows([nc.scalar] * 4, x_scale_tab, x_scales)
+        offs_t = load_list(offs, "offs_t")
+        w_word_raw = [tile([P, 2 * H], U8, "w_word_raw%d" % i) for i in range(3)]
+        nc.sync.dma_start(out=w_word_raw[0][:].bitcast(I32), in_=w1_words[0].bitcast(I32))
+        x_word_tab = tile([P, T], I32, "x_word_tab")
+        nc.sync.dma_start(out=x_word_tab[:], in_=x_words[0].rearrange("p n r -> p (n r)").bitcast(I32))
+        load_scale_rows([nc.sync, nc.sync, nc.gpsimd, nc.gpsimd], w_scale_raw[0], w1_scales)
+        n1_t = load_list(n1, "n1_t")
+        n2_t = load_list(n2, "n2_t")
+        n3_t = load_list(n3, "n3_t")
+        nc.gpsimd.dma_start(out=w_word_raw[2][:].bitcast(I32), in_=w3_words[0].bitcast(I32))
+        nc.gpsimd.dma_start(out=w_word_raw[1][:].bitcast(I32), in_=w2_words[0].bitcast(I32))
+        n4_t = load_list(n4, "n4_t")
+        gm_t = tile([P, PACK], F32, "gm_t")
+        gn_t = tile([P, PACK], F32, "gn_t")
+        nc.sync.dma_start(out=gm_t[:], in_=gm.rearrange("(p t) o -> p (t o)", t=PACK))
+        nc.sync.dma_start(out=gn_t[:], in_=gn.rearrange("(p t) o -> p (t o)", t=PACK))
+        load_scale_rows([nc.sync] * 4, w_scale_raw[2], w3_scales)
+        load_scale_rows([nc.sync] * 4, w_scale_raw[1], w2_scales)
+        n6_t = load_list(n6, "n6_t")
+        n5_t = load_list(n5, "n5_t")
+
+        y_win = tiles([P, 2 * S], F32, "y_win")
+        h_win = tiles([P, S], F32, "h_win")
+        for win in y_win:
+            nc.vector.memset(win[:, S:], 0.0)
+
+        w_words = [tile([P, PACK, 2 * P], U8, "w_words%d" % i) for i in range(3)]
+        w_scales = [tile([P, PACK, P], U8, "w_scales%d" % i) for i in range(3)]
+
+        def deal_words(i):
+            nc.vector.tensor_copy(
+                out=w_words[i][:].rearrange("p t (m b) -> p t m b", b=2),
+                in_=w_word_raw[i][:].rearrange("p (m t b) -> p t m b", t=PACK, b=2),
+            )
+
+        def deal_scales(i):
+            nc.vector.tensor_copy(out=w_scales[i][:], in_=w_scale_raw[i][:].rearrange("p (m t) -> p t m", t=PACK))
+
+        def product(bank, i, t, codes, scales, start, stop):
+            nc.tensor.matmul_mx(
+                out=bank[:], lhsT=w_words[i][:, t, :].bitcast(FP4X4), lhsT_scale=w_scales[i][:, t, :],
+                rhs=codes[:].bitcast(FP8X4), rhs_scale=scales[:], start=start, stop=stop,
+            )
+
+        xq_scales = tile([P, S], U8, "xq_scales")
+        xq_words = tile([P, S], U32, "xq_words")
+        nc.vector.tensor_copy(xq_scales[:], x_scale_tab[:].indirect(offs_t[:]))
+        deal_words(0)
+        nc.vector.tensor_copy(xq_words[:], x_word_tab[:].bitcast(U32).indirect(offs_t[:]))
+        deal_scales(0)
+        deal_words(2)
+        deal_words(1)
+
+        st_win = tiles([P, 2 * S], F32, "st_win")
+        gy = tile([P, PACK, S], F32, "gy")
+        y_bank = [ps.tile([P, S], F32, name="y_bank%d" % t) for t in range(PACK)]
+        for t in range(PACK):
+            product(y_bank[t], 0, t, xq_words, xq_scales, True, True)
+            copies = [y_win[t][:, :S], st_win[t][:, S:]]
+            for dst in copies if t == 0 else reversed(copies):
+                nc.scalar.copy(out=dst, in_=y_bank[t][:])
+
+        pa = tiles([P, W], F32, "pa")
+        minus_pb = tiles([P, W], F32, "minus_pb")
+        pa75 = tiles([P, W], F32, "pa75")
+        pb75 = tiles([P, W], F32, "pb75")
+        dt = tiles([P, S], F32, "dt")
+        gate = tile([P, PACK, S], F32, "gate")
+        z_bf = tile([P, S, PACK], BF16, "z_bf")
+        z2_bf = tile([P, S, PACK], BF16, "z2_bf")
+
+        for t in range(PACK):
+            nc.vector.tensor_copy(pa[t][:], y_win[t][:].indirect(n1_t[:]))
+            nc.vector.tensor_scalar(minus_pb[t][:], y_win[t][:].indirect(n2_t[:]), -1.0, 0.0, ALU.mult, ALU.add)
+            nc.vector.tensor_tensor(st_win[t][:, :S], y_win[t][:].indirect(n3_t[:]), st_win[t][:, S:], ALU.subtract)
+            nc.vector.tensor_tensor(dt[t][:].indirect(n2_t[:]), pa[t][:], minus_pb[t][:], ALU.add)
+            nc.scalar.activation(out=gate[:, t, :], in_=st_win[t][:].indirect(n4_t[:]), func=ACT.Sigmoid)
+            nc.scalar.activation(out=pa75[t][:], in_=pa[t][:], func=ACT.Copy, scale=0.75)
+            nc.scalar.activation(out=pb75[t][:], in_=minus_pb[t][:], func=ACT.Copy, scale=-0.75)
+            nc.scalar.activation(out=gy[:, t, :], in_=y_bank[t][:], func=ACT.Copy, scale=gm_t[:, t : t + 1])
+        deal_scales(2)
+        deal_scales(1)
+        for t in range(PACK):
+            nc.vector.tensor_tensor(dt[t][:].indirect(n1_t[:]), pa75[t][:], pb75[t][:], ALU.add)
+            nc.scalar.activation(out=z_bf[:, :, t], in_=dt[t][:], func=ACT.Copy, scale=gn_t[:, t : t + 1])
+        pairs = "p t (c i) -> p c t i"
+        nc.vector.tensor_tensor(
+            z2_bf[:].rearrange("p (c i) t -> p c t i", i=2), gate[:].rearrange(pairs, i=2), gy[:].rearrange(pairs, i=2), ALU.mult
+        )
+
+        z2_words = tile([P, S], U32, "z2_words")
+        z2_scales = tile([P, S], U8, "z2_scales")
+        z_words = tile([P, S], U32, "z_words")
+        z_scales = tile([P, S], U8, "z_scales")
+
+        def quantize(words, scales, woven, lo, hi):
+            nc.vector.quantize_mx(
+                out=words[:, lo:hi].bitcast(FP8X4), scales=scales[:, lo:hi], in_=woven[:, lo:hi, :].rearrange("p c t -> p (c t)")
+            )
+
+        quantize(z_words, z_scales, z_bf, 0, S // 2)
+        quantize(z2_words, z2_scales, z2_bf, 0, S)
+        quantize(z_words, z_scales, z_bf, S // 2, S)
+
+        h_bank = [ps.tile([P, S], F32, name="h_bank%d" % t) for t in range(PACK)]
+        for t in range(PACK):
+            product(h_bank[t], 2, t, z2_words, z2_scales, True, False)
+            product(h_bank[t], 1, t, z_words, z_scales, False, True)
+            nc.scalar.copy(out=h_win[t][:, :S], in_=h_bank[t][:])
+
+        out_rows = out_0.rearrange("(p t) c -> p t c", t=PACK)
+        out_words = out_1[0].rearrange("p c r -> p (c r)").bitcast(I32)
+        o_scales = tile([P, S], U8, "o_scales")
+        o_words = tile([P, S], I32, "o_words")
+        res_bf = tile([P, S, PACK], BF16, "res_bf")
+        for lo, hi in CHUNKS:
+            width = hi - lo
+            entries = slice(lo // LANES, hi // LANES)
+            h6 = tile([P, PACK, width], F32, "h6")
+            h56 = tile([P, PACK, width], F32, "h56_%d" % lo)
+            sig = tile([P, PACK, width], F32, "sig_%d" % lo)
+            res = tile([P, PACK, width], F32, "res_%d" % lo)
+
+            def finish(t):
+                nc.vector.tensor_tensor(res[:, t, :], sig[:, t, :], h_win[t][:, lo:hi], ALU.mult)
+
+            for t in range(PACK):
+                nc.vector.tensor_copy(h6[:, t, :], h_win[t][:].indirect(n6_t[:, entries]))
+            for t in range(PACK):
+                nc.vector.tensor_tensor(h56[:, t, :], h_win[t][:].indirect(n5_t[:, entries]), h6[:, t, :], ALU.subtract)
+                nc.scalar.activation(out=sig[:, t, :], in_=h56[:, t, :], func=ACT.Sigmoid)
+                if t > 0:
+                    finish(t - 1)
+            finish(PACK - 1)
+            nc.sync.dma_start(out=out_rows[:, :, lo:hi], in_=res[:])
+            woven = res_bf[:, lo:hi, :].rearrange("p (c i) t -> p c t i", i=2)
+            planes = res[:].rearrange(pairs, i=2)
+            if hi < S:
+                nc.scalar.copy(out=woven, in_=planes)
+            else:
+                nc.vector.tensor_copy(out=woven, in_=planes)
+            quantize(o_words, o_scales, res_bf, lo, hi)
+            nc.sync.dma_start(out=out_words[:, lo:hi], in_=o_words[:, lo:hi])
+        for q in range(QUADRANTS):
+            queue = nc.scalar if q % 2 else nc.sync
+            queue.dma_start(out=out_2[0, 4 * q : 4 * q + 4, :].bitcast(I32), in_=o_scales[32 * q : 32 * q + 4, :].bitcast(I32))

@@ -49,29 +49,25 @@ def tile_picked_joinhaarhopdcmp_none_po_kernel(
             return lst
 
         x_scale_tab = tile([P, T], U8, "x_scale_tab")
-        w_scale_raw = [tile([P, H], U8, "w_scale_raw%d" % i) for i in range(3)]
+        w1_scale_raw = tile([P, 1, H], U8, "w1_scale_raw")
+        w23_scale_raw = tile([P, 2, H], U8, "w23_scale_raw")
         nc.vector.memset(x_scale_tab[:].bitcast(I32), 0)
-        for i in range(3):
-            nc.vector.memset(w_scale_raw[i][:].bitcast(I32), 0)
-        load_scale_rows([nc.scalar] * 4, x_scale_tab, x_scales)
+        nc.vector.memset(w1_scale_raw[:].bitcast(I32), 0)
         offs_t = load_list(offs, "offs_t")
-        w_word_raw = [tile([P, 2 * H], U8, "w_word_raw%d" % i) for i in range(3)]
-        nc.sync.dma_start(out=w_word_raw[0][:].bitcast(I32), in_=w1_words[0].bitcast(I32))
+        w1_word_raw = tile([P, 1, 2 * H], U8, "w_word_raw")
+        nc.sync.dma_start(out=w1_word_raw[:, 0, :].bitcast(I32), in_=w1_words[0].bitcast(I32))
+        n1_t = load_list(n1, "n1_t")
         x_word_tab = tile([P, T], I32, "x_word_tab")
         nc.sync.dma_start(out=x_word_tab[:], in_=x_words[0].rearrange("p n r -> p (n r)").bitcast(I32))
-        load_scale_rows([nc.sync, nc.sync, nc.gpsimd, nc.gpsimd], w_scale_raw[0], w1_scales)
-        n1_t = load_list(n1, "n1_t")
+        load_scale_rows([nc.sync] * 4, x_scale_tab, x_scales)
+        load_scale_rows([nc.sync, nc.sync, nc.gpsimd, nc.gpsimd], w1_scale_raw[:, 0, :], w1_scales)
         n2_t = load_list(n2, "n2_t")
         n3_t = load_list(n3, "n3_t")
-        nc.gpsimd.dma_start(out=w_word_raw[2][:].bitcast(I32), in_=w3_words[0].bitcast(I32))
-        nc.gpsimd.dma_start(out=w_word_raw[1][:].bitcast(I32), in_=w2_words[0].bitcast(I32))
         n4_t = load_list(n4, "n4_t")
         gm_t = tile([P, PACK], F32, "gm_t")
         gn_t = tile([P, PACK], F32, "gn_t")
         nc.sync.dma_start(out=gm_t[:], in_=gm.rearrange("(p t) o -> p (t o)", t=PACK))
         nc.sync.dma_start(out=gn_t[:], in_=gn.rearrange("(p t) o -> p (t o)", t=PACK))
-        load_scale_rows([nc.sync] * 4, w_scale_raw[2], w3_scales)
-        load_scale_rows([nc.sync] * 4, w_scale_raw[1], w2_scales)
         n6_t = load_list(n6, "n6_t")
         n5_t = load_list(n5, "n5_t")
 
@@ -79,42 +75,60 @@ def tile_picked_joinhaarhopdcmp_none_po_kernel(
         h_win = tiles([P, S], F32, "h_win")
         for win in y_win:
             nc.vector.memset(win[:, S:], 0.0)
+        nc.vector.memset(w23_scale_raw[:].bitcast(I32), 0)
+        load_scale_rows([nc.sync] * 4, w23_scale_raw[:, 1, :], w3_scales)
+        load_scale_rows([nc.sync] * 4, w23_scale_raw[:, 0, :], w2_scales)
 
-        w_words = [tile([P, PACK, 2 * P], U8, "w_words%d" % i) for i in range(3)]
-        w_scales = [tile([P, PACK, P], U8, "w_scales%d" % i) for i in range(3)]
-
-        def deal_words(i):
+        def deal_words(raw, lo, hi, name):
+            dealt = tile([P, raw.shape[1], hi - lo, 2 * P], U8, name)
             nc.vector.tensor_copy(
-                out=w_words[i][:].rearrange("p t (m b) -> p t m b", b=2),
-                in_=w_word_raw[i][:].rearrange("p (m t b) -> p t m b", t=PACK, b=2),
+                out=dealt[:].rearrange("p w t (m b) -> p w t m b", b=2),
+                in_=raw[:].rearrange("p w (m t b) -> p w t m b", t=PACK, b=2)[:, :, lo:hi],
             )
+            return dealt
 
-        def deal_scales(i):
-            nc.vector.tensor_copy(out=w_scales[i][:], in_=w_scale_raw[i][:].rearrange("p (m t) -> p t m", t=PACK))
+        def deal_scales(raw, lo, hi, name):
+            dealt = tile([P, raw.shape[1], hi - lo, P], U8, name)
+            nc.vector.tensor_copy(out=dealt[:], in_=raw[:].rearrange("p w (m t) -> p w t m", t=PACK)[:, :, lo:hi])
+            return dealt
 
-        def product(bank, i, t, codes, scales, start, stop):
+        def product(bank, w_words, w_scales, codes, scales, start, stop):
             nc.tensor.matmul_mx(
-                out=bank[:], lhsT=w_words[i][:, t, :].bitcast(FP4X4), lhsT_scale=w_scales[i][:, t, :],
-                rhs=codes[:].bitcast(FP8X4), rhs_scale=scales[:], start=start, stop=stop,
+                out=bank, lhsT=w_words.bitcast(FP4X4), lhsT_scale=w_scales,
+                rhs=codes.bitcast(FP8X4), rhs_scale=scales, start=start, stop=stop,
             )
 
-        xq_scales = tile([P, S], U8, "xq_scales")
-        xq_words = tile([P, S], U32, "xq_words")
-        nc.vector.tensor_copy(xq_scales[:], x_scale_tab[:].indirect(offs_t[:]))
-        deal_words(0)
-        nc.vector.tensor_copy(xq_words[:], x_word_tab[:].bitcast(U32).indirect(offs_t[:]))
-        deal_scales(0)
-        deal_words(2)
-        deal_words(1)
+        w1_dealt = deal_words(w1_word_raw, 0, PACK, "w1_dealt")
+        w1_scale_dealt = deal_scales(w1_scale_raw, 0, PACK, "w1_scale_dealt")
+        xq_scales = [tile([P, S // 2], U8, name) for name in ("xq_scales0", "w1_scale_raw")]
+        xq_words = [tile([P, S // 2], U32, "xq_words%d" % j) for j in range(2)]
+        halves = (slice(0, S // 2), slice(S // 2, S))
+        for j, cols in enumerate(halves):
+            entries = slice(cols.start // LANES, cols.stop // LANES)
+            nc.vector.tensor_copy(xq_words[j][:], x_word_tab[:].bitcast(U32).indirect(offs_t[:, entries]))
+            nc.vector.tensor_copy(xq_scales[j][:], x_scale_tab[:].indirect(offs_t[:, entries]))
+        w23_word_raw = tile([P, 2, 2 * H], U8, "w_word_raw")
+        nc.sync.dma_start(out=w23_word_raw[:, 0, :].bitcast(I32), in_=w2_words[0].bitcast(I32))
+        nc.sync.dma_start(out=w23_word_raw[:, 1, :].bitcast(I32), in_=w3_words[0].bitcast(I32))
 
+        first_words = deal_words(w23_word_raw, 0, 1, "x_scale_tab")
         st_win = tiles([P, 2 * S], F32, "st_win")
         gy = tile([P, PACK, S], F32, "gy")
-        y_bank = [ps.tile([P, S], F32, name="y_bank%d" % t) for t in range(PACK)]
+        y_parts = []
         for t in range(PACK):
-            product(y_bank[t], 0, t, xq_words, xq_scales, True, True)
+            if t == 0:
+                parts = [(ps.tile([P, S // 2], F32, name="y_bank0_%d" % j), cols) for j, cols in enumerate(halves)]
+                targets = [bank[:] for bank, cols in parts]
+            else:
+                parts = [(ps.tile([P, S], F32, name="y_bank%d" % t), slice(0, S))]
+                targets = [parts[0][0][:, cols] for cols in halves]
+            for j in range(2):
+                product(targets[j], w1_dealt[:, 0, t, :], w1_scale_dealt[:, 0, t, :], xq_words[j][:], xq_scales[j][:], True, True)
+            y_parts.append(parts)
             copies = [y_win[t][:, :S], st_win[t][:, S:]]
             for dst in copies if t == 0 else reversed(copies):
-                nc.scalar.copy(out=dst, in_=y_bank[t][:])
+                for bank, cols in parts:
+                    nc.scalar.copy(out=dst[:, cols], in_=bank[:])
 
         pa = tiles([P, W], F32, "pa")
         minus_pb = tiles([P, W], F32, "minus_pb")
@@ -133,9 +147,9 @@ def tile_picked_joinhaarhopdcmp_none_po_kernel(
             nc.scalar.activation(out=gate[:, t, :], in_=st_win[t][:].indirect(n4_t[:]), func=ACT.Sigmoid)
             nc.scalar.activation(out=pa75[t][:], in_=pa[t][:], func=ACT.Copy, scale=0.75)
             nc.scalar.activation(out=pb75[t][:], in_=minus_pb[t][:], func=ACT.Copy, scale=-0.75)
-            nc.scalar.activation(out=gy[:, t, :], in_=y_bank[t][:], func=ACT.Copy, scale=gm_t[:, t : t + 1])
-        deal_scales(2)
-        deal_scales(1)
+            for bank, cols in y_parts[t]:
+                nc.scalar.activation(out=gy[:, t, cols], in_=bank[:], func=ACT.Copy, scale=gm_t[:, t : t + 1])
+        first_scales = deal_scales(w23_scale_raw, 0, 1, "minus_pb0")
         for t in range(PACK):
             nc.vector.tensor_tensor(dt[t][:].indirect(n1_t[:]), pa75[t][:], pb75[t][:], ALU.add)
             nc.scalar.activation(out=z_bf[:, :, t], in_=dt[t][:], func=ACT.Copy, scale=gn_t[:, t : t + 1])
@@ -158,11 +172,14 @@ def tile_picked_joinhaarhopdcmp_none_po_kernel(
         quantize(z2_words, z2_scales, z2_bf, 0, S)
         quantize(z_words, z_scales, z_bf, S // 2, S)
 
-        h_bank = [ps.tile([P, S], F32, name="h_bank%d" % t) for t in range(PACK)]
+        rest_words = deal_words(w23_word_raw, 1, PACK, "z2_bf")
+        rest_scales = deal_scales(w23_scale_raw, 1, PACK, "z_bf")
         for t in range(PACK):
-            product(h_bank[t], 2, t, z2_words, z2_scales, True, False)
-            product(h_bank[t], 1, t, z_words, z_scales, False, True)
-            nc.scalar.copy(out=h_win[t][:, :S], in_=h_bank[t][:])
+            bank = ps.tile([P, S], F32, name="h_bank%d" % t if t + 1 < PACK else "y_bank0_1")
+            words, scales, slot = (first_words, first_scales, 0) if t == 0 else (rest_words, rest_scales, t - 1)
+            product(bank[:], words[:, 1, slot, :], scales[:, 1, slot, :], z2_words[:], z2_scales[:], True, False)
+            product(bank[:], words[:, 0, slot, :], scales[:, 0, slot, :], z_words[:], z_scales[:], False, True)
+            nc.scalar.copy(out=h_win[t][:, :S], in_=bank[:])
 
         out_rows = out_0.rearrange("(p t) c -> p t c", t=PACK)
         out_words = out_1[0].rearrange("p c r -> p (c r)").bitcast(I32)

@@ -111,7 +111,6 @@ def tile_picked_joinhaarhopdcmp_none_po_kernel(
         nc.sync.dma_start(out=w23_word_raw[:, 0, :].bitcast(I32), in_=w2_words[0].bitcast(I32))
         nc.sync.dma_start(out=w23_word_raw[:, 1, :].bitcast(I32), in_=w3_words[0].bitcast(I32))
 
-        first_words = deal_words(w23_word_raw, 0, 1, "x_scale_tab")
         st_win = tiles([P, 2 * S], F32, "st_win")
         gy = tile([P, PACK, S], F32, "gy")
         y_parts = []
@@ -149,6 +148,7 @@ def tile_picked_joinhaarhopdcmp_none_po_kernel(
             nc.scalar.activation(out=pb75[t][:], in_=minus_pb[t][:], func=ACT.Copy, scale=-0.75)
             for bank, cols in y_parts[t]:
                 nc.scalar.activation(out=gy[:, t, cols], in_=bank[:], func=ACT.Copy, scale=gm_t[:, t : t + 1])
+        first_words = deal_words(w23_word_raw, 0, 1, "pa0")
         first_scales = deal_scales(w23_scale_raw, 0, 1, "minus_pb0")
         for t in range(PACK):
             nc.vector.tensor_tensor(dt[t][:].indirect(n1_t[:]), pa75[t][:], pb75[t][:], ALU.add)
@@ -195,7 +195,8 @@ def tile_picked_joinhaarhopdcmp_none_po_kernel(
             res = tile([P, PACK, width], F32, "res_%d" % lo)
 
             def finish(t):
-                nc.vector.tensor_tensor(res[:, t, :], sig[:, t, :], h_win[t][:, lo:hi], ALU.mult)
+                engine = nc.gpsimd if hi < S else nc.vector
+                engine.tensor_tensor(res[:, t, :], sig[:, t, :], h_win[t][:, lo:hi], ALU.mult)
 
             for t in range(PACK):
                 nc.vector.tensor_copy(h6[:, t, :], h_win[t][:].indirect(n6_t[:, entries]))

@@ -20,7 +20,6 @@ P = 128
 PACK = 4
 QUADRANTS = 4
 LANES = 16
-CHUNKS = ((0, 256), (256, 384), (384, 512))
 
 
 def load_scale_rows(queues, plane, rows):
@@ -121,7 +120,7 @@ def tile_picked_joinhaarhopdcmp_none_po_kernel(
             else:
                 parts = [(ps.tile([P, S], F32, name="y_bank%d" % t), slice(0, S))]
                 targets = [parts[0][0][:, cols] for cols in halves]
-            for j in range(2):
+            for j in (0, 1) if t == 0 else (1, 0):
                 product(targets[j], w1_dealt[:, 0, t, :], w1_scale_dealt[:, 0, t, :], xq_words[j][:], xq_scales[j][:], True, True)
             y_parts.append(parts)
             copies = [y_win[t][:, :S], st_win[t][:, S:]]
@@ -186,35 +185,36 @@ def tile_picked_joinhaarhopdcmp_none_po_kernel(
         o_scales = tile([P, S], U8, "o_scales")
         o_words = tile([P, S], I32, "o_words")
         res_bf = tile([P, S, PACK], BF16, "res_bf")
-        for lo, hi in CHUNKS:
-            width = hi - lo
-            entries = slice(lo // LANES, hi // LANES)
-            h6 = tile([P, PACK, width], F32, "h6")
-            h56 = tile([P, PACK, width], F32, "h56_%d" % lo)
-            sig = tile([P, PACK, width], F32, "sig_%d" % lo)
-            res = tile([P, PACK, width], F32, "res_%d" % lo)
+        h6 = [tile([P, PACK, S // 2], F32, "h6_%d" % j) for j in range(2)]
+        for j, cols in enumerate(halves):
+            lo, hi = cols.start, cols.stop
+            h56 = tile([P, PACK, S // 2], F32, "h56" if j == 0 else "h6_0")
+            sig = tile([P, PACK, S // 2], F32, "sig_%d" % j)
+            res = tile([P, PACK, S // 2], F32, "res_%d" % j)
 
             def finish(t):
-                engine = nc.gpsimd if hi < S else nc.vector
-                engine.tensor_tensor(res[:, t, :], sig[:, t, :], h_win[t][:, lo:hi], ALU.mult)
+                nc.vector.tensor_tensor(res[:, t, :], sig[:, t, :], h_win[t][:, cols], ALU.mult)
 
             for t in range(PACK):
-                nc.vector.tensor_copy(h6[:, t, :], h_win[t][:].indirect(n6_t[:, entries]))
-            for t in range(PACK):
-                nc.vector.tensor_tensor(h56[:, t, :], h_win[t][:].indirect(n5_t[:, entries]), h6[:, t, :], ALU.subtract)
+                if j == 0:
+                    for k, part in enumerate(halves):
+                        nc.vector.tensor_copy(h6[k][:, t, :], h_win[t][:].indirect(n6_t[:, part.start // LANES : part.stop // LANES]))
+                nc.vector.tensor_tensor(
+                    h56[:, t, :], h_win[t][:].indirect(n5_t[:, lo // LANES : hi // LANES]), h6[j][:, t, :], ALU.subtract
+                )
                 nc.scalar.activation(out=sig[:, t, :], in_=h56[:, t, :], func=ACT.Sigmoid)
                 if t > 0:
                     finish(t - 1)
             finish(PACK - 1)
-            nc.sync.dma_start(out=out_rows[:, :, lo:hi], in_=res[:])
-            woven = res_bf[:, lo:hi, :].rearrange("p (c i) t -> p c t i", i=2)
+            nc.sync.dma_start(out=out_rows[:, :, cols], in_=res[:])
+            split = S // 2 if j == 0 else S // 8
+            woven = res_bf[:, cols, :].rearrange("p (c i) t -> p c t i", i=2)
             planes = res[:].rearrange(pairs, i=2)
-            if hi < S:
-                nc.scalar.copy(out=woven, in_=planes)
-            else:
-                nc.vector.tensor_copy(out=woven, in_=planes)
+            nc.scalar.copy(out=woven[:, : split // 2], in_=planes[:, : split // 2])
+            if j == 1:
+                nc.vector.tensor_copy(out=woven[:, split // 2 :], in_=planes[:, split // 2 :])
             quantize(o_words, o_scales, res_bf, lo, hi)
-            nc.sync.dma_start(out=out_words[:, lo:hi], in_=o_words[:, lo:hi])
+            nc.sync.dma_start(out=out_words[:, cols], in_=o_words[:, cols])
         for q in range(QUADRANTS):
             queue = nc.scalar if q % 2 else nc.sync
             queue.dma_start(out=out_2[0, 4 * q : 4 * q + 4, :].bitcast(I32), in_=o_scales[32 * q : 32 * q + 4, :].bitcast(I32))

@@ -19,12 +19,25 @@ ACT = mybir.ActivationFunctionType
 P = 128
 PACK = 4
 QUADRANTS = 4
-LANES = 16
+ENTRIES_A_COLUMN = 16
+W2, W3 = 0, 1
+LAST_WEAVE_ON_SCALAR = 64
+WALK_ROW_TILES = "p t (c i) -> p c t i"
+WALK_WOVEN = "p (c i) t -> p c t i"
 
 
-def load_scale_rows(queues, plane, rows):
+def entries(cols):
+    return slice(cols.start // ENTRIES_A_COLUMN, cols.stop // ENTRIES_A_COLUMN)
+
+
+def scale_rows(q):
+    return slice(32 * q, 32 * q + 4), slice(4 * q, 4 * q + 4)
+
+
+def load_scales(queues, scale_tile, scales):
     for q in range(QUADRANTS):
-        queues[q].dma_start(out=plane[32 * q : 32 * q + 4, :].bitcast(I32), in_=rows[0, 4 * q : 4 * q + 4, :].bitcast(I32))
+        partitions, rows = scale_rows(q)
+        queues[q].dma_start(out=scale_tile[partitions, :].bitcast(I32), in_=scales[0, rows, :].bitcast(I32))
 
 
 def tile_picked_joinhaarhopdcmp_none_po_kernel(
@@ -32,189 +45,197 @@ def tile_picked_joinhaarhopdcmp_none_po_kernel(
     offs, n1, n2, n3, n4, n5, n6, out_0, out_1, out_2,
 ):
     nc = tc.nc
+    halves = (slice(0, S // 2), slice(S // 2, S))
+    quarters = [slice(q * P, (q + 1) * P) for q in range(S // P)]
     with ExitStack() as ctx:
-        sb = ctx.enter_context(tc.tile_pool(name="sb", bufs=1))
-        ps = ctx.enter_context(tc.psum_pool(name="ps", bufs=1))
+        sbuf = ctx.enter_context(tc.tile_pool(name="sbuf", bufs=1))
+        psum = ctx.enter_context(tc.psum_pool(name="psum", bufs=1))
 
-        def tile(shape, dtype, name):
-            return sb.tile(shape, dtype, name=name, align_bytes=64)
+        def tile(shape, dtype, name, in_place_of=None):
+            return sbuf.tile(shape, dtype, name=name, tag=in_place_of or name, align_bytes=64)
 
-        def tiles(shape, dtype, name):
-            return [tile(shape, dtype, "%s%d" % (name, t)) for t in range(PACK)]
+        def row_tiles(width, name):
+            return [tile([P, width], F32, "%s%d" % (name, t)) for t in range(PACK)]
 
-        def load_list(src, name):
-            lst = tile(list(src.shape), U16, name)
-            nc.sync.dma_start(lst[:], src)
-            return lst
+        def load_list(lists, name):
+            list_tile = tile(list(lists.shape), U16, name)
+            nc.sync.dma_start(list_tile[:], lists)
+            return list_tile
 
-        x_scale_tab = tile([P, T], U8, "x_scale_tab")
-        w1_scale_raw = tile([P, 1, H], U8, "w1_scale_raw")
-        w23_scale_raw = tile([P, 2, H], U8, "w23_scale_raw")
-        nc.vector.memset(x_scale_tab[:].bitcast(I32), 0)
-        nc.vector.memset(w1_scale_raw[:].bitcast(I32), 0)
-        offs_t = load_list(offs, "offs_t")
-        w1_word_raw = tile([P, 1, 2 * H], U8, "w_word_raw")
-        nc.sync.dma_start(out=w1_word_raw[:, 0, :].bitcast(I32), in_=w1_words[0].bitcast(I32))
-        n1_t = load_list(n1, "n1_t")
-        x_word_tab = tile([P, T], I32, "x_word_tab")
-        nc.sync.dma_start(out=x_word_tab[:], in_=x_words[0].rearrange("p n r -> p (n r)").bitcast(I32))
-        load_scale_rows([nc.sync] * 4, x_scale_tab, x_scales)
-        load_scale_rows([nc.sync, nc.sync, nc.gpsimd, nc.gpsimd], w1_scale_raw[:, 0, :], w1_scales)
-        n2_t = load_list(n2, "n2_t")
-        n3_t = load_list(n3, "n3_t")
-        n4_t = load_list(n4, "n4_t")
-        gm_t = tile([P, PACK], F32, "gm_t")
-        gn_t = tile([P, PACK], F32, "gn_t")
-        nc.sync.dma_start(out=gm_t[:], in_=gm.rearrange("(p t) o -> p (t o)", t=PACK))
-        nc.sync.dma_start(out=gn_t[:], in_=gn.rearrange("(p t) o -> p (t o)", t=PACK))
-        n6_t = load_list(n6, "n6_t")
-        n5_t = load_list(n5, "n5_t")
-
-        y_win = tiles([P, 2 * S], F32, "y_win")
-        h_win = tiles([P, S], F32, "h_win")
-        for win in y_win:
-            nc.vector.memset(win[:, S:], 0.0)
-        nc.vector.memset(w23_scale_raw[:].bitcast(I32), 0)
-        load_scale_rows([nc.sync] * 4, w23_scale_raw[:, 1, :], w3_scales)
-        load_scale_rows([nc.sync] * 4, w23_scale_raw[:, 0, :], w2_scales)
-
-        def deal_words(raw, lo, hi, name):
-            dealt = tile([P, raw.shape[1], hi - lo, 2 * P], U8, name)
+        def deal_words(raw, name, in_place_of=None):
+            dealt = tile([P, raw.shape[1], PACK, 2 * P], U8, name, in_place_of)
             nc.vector.tensor_copy(
                 out=dealt[:].rearrange("p w t (m b) -> p w t m b", b=2),
-                in_=raw[:].rearrange("p w (m t b) -> p w t m b", t=PACK, b=2)[:, :, lo:hi],
+                in_=raw[:].rearrange("p w (m t b) -> p w t m b", t=PACK, b=2),
             )
             return dealt
 
-        def deal_scales(raw, lo, hi, name):
-            dealt = tile([P, raw.shape[1], hi - lo, P], U8, name)
-            nc.vector.tensor_copy(out=dealt[:], in_=raw[:].rearrange("p w (m t) -> p w t m", t=PACK)[:, :, lo:hi])
+        def deal_scales(raw, first, last, name, in_place_of=None):
+            dealt = tile([P, raw.shape[1], last - first, P], U8, name, in_place_of)
+            nc.vector.tensor_copy(out=dealt[:], in_=raw[:].rearrange("p w (m t) -> p w t m", t=PACK)[:, :, first:last])
             return dealt
 
-        def product(bank, w_words, w_scales, codes, scales, start, stop):
+        def product(target, weight_words, weight_scales, words, scales, start, stop):
             nc.tensor.matmul_mx(
-                out=bank, lhsT=w_words.bitcast(FP4X4), lhsT_scale=w_scales,
-                rhs=codes.bitcast(FP8X4), rhs_scale=scales, start=start, stop=stop,
+                out=target, lhsT=weight_words.bitcast(FP4X4), lhsT_scale=weight_scales,
+                rhs=words.bitcast(FP8X4), rhs_scale=scales, start=start, stop=stop,
             )
 
-        w1_dealt = deal_words(w1_word_raw, 0, PACK, "w1_dealt")
-        w1_scale_dealt = deal_scales(w1_scale_raw, 0, PACK, "w1_scale_dealt")
-        xq_scales = [tile([P, S // 2], U8, name) for name in ("xq_scales0", "w1_scale_raw")]
-        xq_words = [tile([P, S // 2], U32, "xq_words%d" % j) for j in range(2)]
-        halves = (slice(0, S // 2), slice(S // 2, S))
-        for j, cols in enumerate(halves):
-            entries = slice(cols.start // LANES, cols.stop // LANES)
-            nc.vector.tensor_copy(xq_words[j][:], x_word_tab[:].bitcast(U32).indirect(offs_t[:, entries]))
-            nc.vector.tensor_copy(xq_scales[j][:], x_scale_tab[:].indirect(offs_t[:, entries]))
-        w23_word_raw = tile([P, 2, 2 * H], U8, "w_word_raw")
-        nc.sync.dma_start(out=w23_word_raw[:, 0, :].bitcast(I32), in_=w2_words[0].bitcast(I32))
-        nc.sync.dma_start(out=w23_word_raw[:, 1, :].bitcast(I32), in_=w3_words[0].bitcast(I32))
+        def quantize(words, scales, woven, cols):
+            nc.vector.quantize_mx(
+                out=words[:, cols].bitcast(FP8X4), scales=scales[:, cols], in_=woven[:, cols, :].rearrange("p c t -> p (c t)")
+            )
 
-        st_win = tiles([P, 2 * S], F32, "st_win")
-        gy = tile([P, PACK, S], F32, "gy")
-        y_parts = []
+        x_scale_table = tile([P, T], U8, "x_scale_table")
+        w1_scale_raw = tile([P, 1, H], U8, "w1_scale_raw")
+        w23_scale_raw = tile([P, 2, H], U8, "w23_scale_raw")
+        nc.vector.memset(x_scale_table[:].bitcast(I32), 0)
+        nc.vector.memset(w1_scale_raw[:].bitcast(I32), 0)
+        offs_list = load_list(offs, "offs_list")
+        w1_word_raw = tile([P, 1, 2 * H], U8, "w1_word_raw")
+        nc.sync.dma_start(out=w1_word_raw[:, 0, :].bitcast(I32), in_=w1_words[0].bitcast(I32))
+        n1_list = load_list(n1, "n1_list")
+        x_word_table = tile([P, T], I32, "x_word_table")
+        nc.sync.dma_start(out=x_word_table[:], in_=x_words[0].rearrange("p n r -> p (n r)").bitcast(I32))
+        load_scales([nc.sync] * QUADRANTS, x_scale_table, x_scales)
+        load_scales([nc.sync, nc.sync, nc.gpsimd, nc.gpsimd], w1_scale_raw[:, 0, :], w1_scales)
+        n2_list = load_list(n2, "n2_list")
+        n3_list = load_list(n3, "n3_list")
+        w23_word_raw = tile([P, 2, 2 * N], U8, "w23_word_raw")
+        nc.sync.dma_start(out=w23_word_raw[:, W2, :].bitcast(I32), in_=w2_words[0].bitcast(I32))
+        nc.sync.dma_start(out=w23_word_raw[:, W3, :].bitcast(I32), in_=w3_words[0].bitcast(I32))
+        n4_list = load_list(n4, "n4_list")
+        gm_rows = tile([P, PACK], F32, "gm_rows")
+        gn_rows = tile([P, PACK], F32, "gn_rows")
+        nc.sync.dma_start(out=gm_rows[:], in_=gm.rearrange("(p t) o -> p (t o)", t=PACK))
+        nc.sync.dma_start(out=gn_rows[:], in_=gn.rearrange("(p t) o -> p (t o)", t=PACK))
+        n6_list = load_list(n6, "n6_list")
+        n5_list = load_list(n5, "n5_list")
+
+        y_window = row_tiles(2 * S, "y_window")
+        h_window = row_tiles(S, "h_window")
+        for window in y_window:
+            nc.vector.memset(window[:, S:], 0.0)
+        nc.vector.memset(w23_scale_raw[:].bitcast(I32), 0)
+        load_scales([nc.sync] * QUADRANTS, w23_scale_raw[:, W3, :], w3_scales)
+        load_scales([nc.sync] * QUADRANTS, w23_scale_raw[:, W2, :], w2_scales)
+
+        w1_word_parts = deal_words(w1_word_raw, "w1_word_parts")
+        w1_scale_parts = deal_scales(w1_scale_raw, 0, PACK, "w1_scale_parts")
+        picked_scales = [tile([P, S // 2], U8, "picked_scales0"), tile([P, S // 2], U8, "picked_scales1", "w1_scale_raw")]
+        picked_words = [tile([P, S // 2], U32, "picked_words%d" % j) for j in range(len(halves))]
+        for j, cols in enumerate(halves):
+            nc.vector.tensor_copy(picked_words[j][:], x_word_table[:].bitcast(U32).indirect(offs_list[:, entries(cols)]))
+            nc.vector.tensor_copy(picked_scales[j][:], x_scale_table[:].indirect(offs_list[:, entries(cols)]))
+        w23_word_parts = deal_words(w23_word_raw, "w23_word_parts", "x_scale_table")
+
+        st_window = row_tiles(2 * S, "st_window")
+        gm_y = tile([P, PACK, S], F32, "gm_y")
+        y_banks = []
         for t in range(PACK):
             if t == 0:
-                parts = [(ps.tile([P, S // 2], F32, name="y_bank0_%d" % j), cols) for j, cols in enumerate(halves)]
-                targets = [bank[:] for bank, cols in parts]
+                banks = [(psum.tile([P, S // 2], F32, name="y_bank0_%d" % j), cols) for j, cols in enumerate(halves)]
+                targets = [bank[:] for bank, cols in banks]
             else:
-                parts = [(ps.tile([P, S], F32, name="y_bank%d" % t), slice(0, S))]
-                targets = [parts[0][0][:, cols] for cols in halves]
+                banks = [(psum.tile([P, S], F32, name="y_bank%d" % t), slice(0, S))]
+                targets = [banks[0][0][:, cols] for cols in halves]
             for j in (0, 1) if t == 0 else (1, 0):
-                product(targets[j], w1_dealt[:, 0, t, :], w1_scale_dealt[:, 0, t, :], xq_words[j][:], xq_scales[j][:], True, True)
-            y_parts.append(parts)
-            copies = [y_win[t][:, :S], st_win[t][:, S:]]
-            for dst in copies if t == 0 else reversed(copies):
-                for bank, cols in parts:
-                    nc.scalar.copy(out=dst[:, cols], in_=bank[:])
+                product(targets[j], w1_word_parts[:, 0, t, :], w1_scale_parts[:, 0, t, :], picked_words[j][:], picked_scales[j][:], True, True)
+            y_banks.append(banks)
+            copies = [y_window[t][:, :S], st_window[t][:, S:]]
+            for copy in copies if t == 0 else reversed(copies):
+                for bank, cols in banks:
+                    nc.scalar.copy(out=copy[:, cols], in_=bank[:])
 
-        pa = tiles([P, W], F32, "pa")
-        minus_pb = tiles([P, W], F32, "minus_pb")
-        pa75 = tiles([P, W], F32, "pa75")
-        pb75 = tiles([P, W], F32, "pb75")
-        dt = tiles([P, S], F32, "dt")
-        gate = tile([P, PACK, S], F32, "gate")
-        z_bf = tile([P, S, PACK], BF16, "z_bf")
-        z2_bf = tile([P, S, PACK], BF16, "z2_bf")
+        pa = row_tiles(W, "pa")
+        minus_pb = row_tiles(W, "minus_pb")
+        pa75 = row_tiles(W, "pa75")
+        pb75 = row_tiles(W, "pb75")
+        dt = row_tiles(S, "dt")
+        z2_gate = tile([P, PACK, S], F32, "z2_gate")
+        z_woven = tile([P, S, PACK], BF16, "z_woven")
+        z2_woven = tile([P, S, PACK], BF16, "z2_woven")
 
         for t in range(PACK):
-            nc.vector.tensor_copy(pa[t][:], y_win[t][:].indirect(n1_t[:]))
-            nc.vector.tensor_scalar(minus_pb[t][:], y_win[t][:].indirect(n2_t[:]), -1.0, 0.0, ALU.mult, ALU.add)
-            nc.vector.tensor_tensor(st_win[t][:, :S], y_win[t][:].indirect(n3_t[:]), st_win[t][:, S:], ALU.subtract)
-            nc.vector.tensor_tensor(dt[t][:].indirect(n2_t[:]), pa[t][:], minus_pb[t][:], ALU.add)
-            nc.scalar.activation(out=gate[:, t, :], in_=st_win[t][:].indirect(n4_t[:]), func=ACT.Sigmoid)
+            nc.vector.tensor_copy(pa[t][:], y_window[t][:].indirect(n1_list[:]))
+            nc.vector.tensor_scalar(minus_pb[t][:], y_window[t][:].indirect(n2_list[:]), -1.0, 0.0, ALU.mult, ALU.add)
+            nc.vector.tensor_tensor(st_window[t][:, :S], y_window[t][:].indirect(n3_list[:]), st_window[t][:, S:], ALU.subtract)
+            nc.vector.tensor_tensor(dt[t][:].indirect(n2_list[:]), pa[t][:], minus_pb[t][:], ALU.add)
+            nc.scalar.activation(out=z2_gate[:, t, :], in_=st_window[t][:].indirect(n4_list[:]), func=ACT.Sigmoid)
             nc.scalar.activation(out=pa75[t][:], in_=pa[t][:], func=ACT.Copy, scale=0.75)
             nc.scalar.activation(out=pb75[t][:], in_=minus_pb[t][:], func=ACT.Copy, scale=-0.75)
-            for bank, cols in y_parts[t]:
-                nc.scalar.activation(out=gy[:, t, cols], in_=bank[:], func=ACT.Copy, scale=gm_t[:, t : t + 1])
-        first_words = deal_words(w23_word_raw, 0, 1, "pa0")
-        first_scales = deal_scales(w23_scale_raw, 0, 1, "minus_pb0")
+            for bank, cols in y_banks[t]:
+                nc.scalar.activation(out=gm_y[:, t, cols], in_=bank[:], func=ACT.Copy, scale=gm_rows[:, t : t + 1])
+        w23_scale_first = deal_scales(w23_scale_raw, 0, 1, "w23_scale_first", "minus_pb0")
         for t in range(PACK):
-            nc.vector.tensor_tensor(dt[t][:].indirect(n1_t[:]), pa75[t][:], pb75[t][:], ALU.add)
-            nc.scalar.activation(out=z_bf[:, :, t], in_=dt[t][:], func=ACT.Copy, scale=gn_t[:, t : t + 1])
-        pairs = "p t (c i) -> p c t i"
+            nc.vector.tensor_tensor(dt[t][:].indirect(n1_list[:]), pa75[t][:], pb75[t][:], ALU.add)
+            nc.scalar.activation(out=z_woven[:, :, t], in_=dt[t][:], func=ACT.Copy, scale=gn_rows[:, t : t + 1])
         nc.vector.tensor_tensor(
-            z2_bf[:].rearrange("p (c i) t -> p c t i", i=2), gate[:].rearrange(pairs, i=2), gy[:].rearrange(pairs, i=2), ALU.mult
+            z2_woven[:].rearrange(WALK_WOVEN, i=2), z2_gate[:].rearrange(WALK_ROW_TILES, i=2),
+            gm_y[:].rearrange(WALK_ROW_TILES, i=2), ALU.mult,
         )
 
         z2_words = tile([P, S], U32, "z2_words")
         z2_scales = tile([P, S], U8, "z2_scales")
         z_words = tile([P, S], U32, "z_words")
         z_scales = tile([P, S], U8, "z_scales")
+        quantize(z_words, z_scales, z_woven, halves[0])
+        quantize(z2_words, z2_scales, z2_woven, slice(0, S))
+        quantize(z_words, z_scales, z_woven, halves[1])
 
-        def quantize(words, scales, woven, lo, hi):
-            nc.vector.quantize_mx(
-                out=words[:, lo:hi].bitcast(FP8X4), scales=scales[:, lo:hi], in_=woven[:, lo:hi, :].rearrange("p c t -> p (c t)")
-            )
-
-        quantize(z_words, z_scales, z_bf, 0, S // 2)
-        quantize(z2_words, z2_scales, z2_bf, 0, S)
-        quantize(z_words, z_scales, z_bf, S // 2, S)
-
-        rest_words = deal_words(w23_word_raw, 1, PACK, "z2_bf")
-        rest_scales = deal_scales(w23_scale_raw, 1, PACK, "z_bf")
-        for t in range(PACK):
-            bank = ps.tile([P, S], F32, name="h_bank%d" % t if t + 1 < PACK else "y_bank0_1")
-            words, scales, slot = (first_words, first_scales, 0) if t == 0 else (rest_words, rest_scales, t - 1)
-            product(bank[:], words[:, 1, slot, :], scales[:, 1, slot, :], z2_words[:], z2_scales[:], True, False)
-            product(bank[:], words[:, 0, slot, :], scales[:, 0, slot, :], z_words[:], z_scales[:], False, True)
-            nc.scalar.copy(out=h_win[t][:, :S], in_=bank[:])
+        w23_scale_rest = deal_scales(w23_scale_raw, 1, PACK, "w23_scale_rest", "z_woven")
+        free_banks = ("y_bank0_0", "y_bank0_1", "y_bank1", "y_bank2")
+        quarter_banks = [psum.tile([P, P], F32, name="h_bank0_%d" % q, tag=tag) for q, tag in enumerate(free_banks)]
+        for bank, cols in zip(quarter_banks, quarters):
+            product(bank[:], w23_word_parts[:, W3, 0, :], w23_scale_first[:, W3, 0, :], z2_words[:, cols], z2_scales[:, cols], True, False)
+        for bank, cols in zip(quarter_banks, quarters):
+            product(bank[:], w23_word_parts[:, W2, 0, :], w23_scale_first[:, W2, 0, :], z_words[:, cols], z_scales[:, cols], False, True)
+            nc.scalar.copy(out=h_window[0][:, cols], in_=bank[:])
+        for t in range(1, PACK):
+            bank = psum.tile([P, S], F32, name="h_bank%d" % t)
+            product(bank[:], w23_word_parts[:, W3, t, :], w23_scale_rest[:, W3, t - 1, :], z2_words[:], z2_scales[:], True, False)
+            product(bank[:], w23_word_parts[:, W2, t, :], w23_scale_rest[:, W2, t - 1, :], z_words[:], z_scales[:], False, True)
+            nc.scalar.copy(out=h_window[t][:], in_=bank[:])
 
         out_rows = out_0.rearrange("(p t) c -> p t c", t=PACK)
-        out_words = out_1[0].rearrange("p c r -> p (c r)").bitcast(I32)
-        o_scales = tile([P, S], U8, "o_scales")
-        o_words = tile([P, S], I32, "o_words")
-        res_bf = tile([P, S, PACK], BF16, "res_bf")
-        h6 = [tile([P, PACK, S // 2], F32, "h6_%d" % j) for j in range(2)]
+        out_word_rows = out_1[0].rearrange("p c r -> p (c r)").bitcast(I32)
+        out_scales = tile([P, S], U8, "out_scales")
+        out_words = tile([P, S], I32, "out_words")
+        out_woven = tile([P, S, PACK], BF16, "out_woven")
+        h6 = [tile([P, PACK, S // 2], F32, "h6_%d" % j) for j in range(len(halves))]
         for j, cols in enumerate(halves):
-            lo, hi = cols.start, cols.stop
-            h56 = tile([P, PACK, S // 2], F32, "h56" if j == 0 else "h6_0")
-            sig = tile([P, PACK, S // 2], F32, "sig_%d" % j)
-            res = tile([P, PACK, S // 2], F32, "res_%d" % j)
+            first_round = j == 0
+            difference = tile([P, PACK, S // 2], F32, "difference%d" % j, None if first_round else "h6_0")
+            out_gate = tile([P, PACK, S // 2], F32, "out_gate%d" % j)
+            result = tile([P, PACK, S // 2], F32, "result%d" % j)
 
-            def finish(t):
-                nc.vector.tensor_tensor(res[:, t, :], sig[:, t, :], h_win[t][:, cols], ALU.mult)
+            def apply_gate(t):
+                nc.vector.tensor_tensor(result[:, t, :], out_gate[:, t, :], h_window[t][:, cols], ALU.mult)
 
             for t in range(PACK):
-                if j == 0:
-                    for k, part in enumerate(halves):
-                        nc.vector.tensor_copy(h6[k][:, t, :], h_win[t][:].indirect(n6_t[:, part.start // LANES : part.stop // LANES]))
+                if first_round:
+                    for fetched, half in zip(h6, halves):
+                        nc.vector.tensor_copy(fetched[:, t, :], h_window[t][:].indirect(n6_list[:, entries(half)]))
                 nc.vector.tensor_tensor(
-                    h56[:, t, :], h_win[t][:].indirect(n5_t[:, lo // LANES : hi // LANES]), h6[j][:, t, :], ALU.subtract
+                    difference[:, t, :], h_window[t][:].indirect(n5_list[:, entries(cols)]), h6[j][:, t, :], ALU.subtract
                 )
-                nc.scalar.activation(out=sig[:, t, :], in_=h56[:, t, :], func=ACT.Sigmoid)
+                nc.scalar.activation(out=out_gate[:, t, :], in_=difference[:, t, :], func=ACT.Sigmoid)
                 if t > 0:
-                    finish(t - 1)
-            finish(PACK - 1)
-            nc.sync.dma_start(out=out_rows[:, :, cols], in_=res[:])
-            split = S // 2 if j == 0 else S // 8
-            woven = res_bf[:, cols, :].rearrange("p (c i) t -> p c t i", i=2)
-            planes = res[:].rearrange(pairs, i=2)
-            nc.scalar.copy(out=woven[:, : split // 2], in_=planes[:, : split // 2])
-            if j == 1:
-                nc.vector.tensor_copy(out=woven[:, split // 2 :], in_=planes[:, split // 2 :])
-            quantize(o_words, o_scales, res_bf, lo, hi)
-            nc.sync.dma_start(out=out_words[:, cols], in_=o_words[:, cols])
+                    apply_gate(t - 1)
+            apply_gate(PACK - 1)
+            nc.sync.dma_start(out=out_rows[:, :, cols], in_=result[:])
+
+            woven_walk = out_woven[:, cols, :].rearrange(WALK_WOVEN, i=2)
+            result_walk = result[:].rearrange(WALK_ROW_TILES, i=2)
+            if first_round:
+                nc.scalar.copy(out=woven_walk, in_=result_walk)
+            else:
+                pairs_on_scalar = LAST_WEAVE_ON_SCALAR // 2
+                nc.scalar.copy(out=woven_walk[:, :pairs_on_scalar], in_=result_walk[:, :pairs_on_scalar])
+                nc.vector.tensor_copy(out=woven_walk[:, pairs_on_scalar:], in_=result_walk[:, pairs_on_scalar:])
+            quantize(out_words, out_scales, out_woven, cols)
+            nc.sync.dma_start(out=out_word_rows[:, cols], in_=out_words[:, cols])
         for q in range(QUADRANTS):
+            partitions, rows = scale_rows(q)
             queue = nc.scalar if q % 2 else nc.sync
-            queue.dma_start(out=out_2[0, 4 * q : 4 * q + 4, :].bitcast(I32), in_=o_scales[32 * q : 32 * q + 4, :].bitcast(I32))
+            queue.dma_start(out=out_2[0, rows, :].bitcast(I32), in_=out_scales[partitions, :].bitcast(I32))

from contextlib import ExitStack

import concourse.mybir as mybir

K, T, S, H, N, W = 512, 2048, 512, 512, 512, 256
FLOPS = 2 * K * H * S + 2 * 2 * H * N * S

F32 = mybir.dt.float32
BF16 = mybir.dt.bfloat16
I32 = mybir.dt.int32
U32 = mybir.dt.uint32
U16 = mybir.dt.uint16
U8 = mybir.dt.uint8
FP8X4 = mybir.dt.float8_e4m3fn_x4
FP4X4 = mybir.dt.float4_e2m1fn_x4
ALU = mybir.AluOpType
ACT = mybir.ActivationFunctionType

P = 128
PACK = 4
QUADRANTS = 4
ENTRIES_A_COLUMN = 16
W2, W3 = 0, 1
LAST_WEAVE_ON_SCALAR = 64
WALK_ROW_TILES = "p t (c i) -> p c t i"
WALK_WOVEN = "p (c i) t -> p c t i"


def entries(cols):
    return slice(cols.start // ENTRIES_A_COLUMN, cols.stop // ENTRIES_A_COLUMN)


def scale_rows(q):
    return slice(32 * q, 32 * q + 4), slice(4 * q, 4 * q + 4)


def load_scales(queues, scale_tile, scales):
    for q in range(QUADRANTS):
        partitions, rows = scale_rows(q)
        queues[q].dma_start(out=scale_tile[partitions, :].bitcast(I32), in_=scales[0, rows, :].bitcast(I32))


def tile_picked_joinhaarhopdcmp_none_po_kernel(
    tc, x_words, x_scales, w1_words, w1_scales, gn, gm, w2_words, w2_scales, w3_words, w3_scales,
    offs, n1, n2, n3, n4, n5, n6, out_0, out_1, out_2,
):
    nc = tc.nc
    halves = (slice(0, S // 2), slice(S // 2, S))
    quarters = [slice(q * P, (q + 1) * P) for q in range(S // P)]
    with ExitStack() as ctx:
        sbuf = ctx.enter_context(tc.tile_pool(name="sbuf", bufs=1))
        psum = ctx.enter_context(tc.psum_pool(name="psum", bufs=1))

        def tile(shape, dtype, name, in_place_of=None):
            return sbuf.tile(shape, dtype, name=name, tag=in_place_of or name, align_bytes=64)

        def row_tiles(width, name):
            return [tile([P, width], F32, "%s%d" % (name, t)) for t in range(PACK)]

        def load_list(lists, name):
            list_tile = tile(list(lists.shape), U16, name)
            nc.sync.dma_start(list_tile[:], lists)
            return list_tile

        def deal_words(raw, name, in_place_of=None):
            dealt = tile([P, raw.shape[1], PACK, 2 * P], U8, name, in_place_of)
            nc.vector.tensor_copy(
                out=dealt[:].rearrange("p w t (m b) -> p w t m b", b=2),
                in_=raw[:].rearrange("p w (m t b) -> p w t m b", t=PACK, b=2),
            )
            return dealt

        def deal_scales(raw, first, last, name, in_place_of=None):
            dealt = tile([P, raw.shape[1], last - first, P], U8, name, in_place_of)
            nc.vector.tensor_copy(out=dealt[:], in_=raw[:].rearrange("p w (m t) -> p w t m", t=PACK)[:, :, first:last])
            return dealt

        def product(target, weight_words, weight_scales, words, scales, start, stop):
            nc.tensor.matmul_mx(
                out=target, lhsT=weight_words.bitcast(FP4X4), lhsT_scale=weight_scales,
                rhs=words.bitcast(FP8X4), rhs_scale=scales, start=start, stop=stop,
            )

        def quantize(words, scales, woven, cols):
            nc.vector.quantize_mx(
                out=words[:, cols].bitcast(FP8X4), scales=scales[:, cols], in_=woven[:, cols, :].rearrange("p c t -> p (c t)")
            )

        x_scale_table = tile([P, T], U8, "x_scale_table")
        w1_scale_raw = tile([P, 1, H], U8, "w1_scale_raw")
        w23_scale_raw = tile([P, 2, H], U8, "w23_scale_raw")
        nc.vector.memset(x_scale_table[:].bitcast(I32), 0)
        nc.vector.memset(w1_scale_raw[:].bitcast(I32), 0)
        offs_list = load_list(offs, "offs_list")
        w1_word_raw = tile([P, 1, 2 * H], U8, "w1_word_raw")
        nc.sync.dma_start(out=w1_word_raw[:, 0, :].bitcast(I32), in_=w1_words[0].bitcast(I32))
        n1_list = load_list(n1, "n1_list")
        x_word_table = tile([P, T], I32, "x_word_table")
        nc.sync.dma_start(out=x_word_table[:], in_=x_words[0].rearrange("p n r -> p (n r)").bitcast(I32))
        load_scales([nc.sync] * QUADRANTS, x_scale_table, x_scales)
        load_scales([nc.sync, nc.sync, nc.gpsimd, nc.gpsimd], w1_scale_raw[:, 0, :], w1_scales)
        n2_list = load_list(n2, "n2_list")
        n3_list = load_list(n3, "n3_list")
        w23_word_raw = tile([P, 2, 2 * N], U8, "w23_word_raw")
        nc.sync.dma_start(out=w23_word_raw[:, W2, :].bitcast(I32), in_=w2_words[0].bitcast(I32))
        nc.sync.dma_start(out=w23_word_raw[:, W3, :].bitcast(I32), in_=w3_words[0].bitcast(I32))
        n4_list = load_list(n4, "n4_list")
        gm_rows = tile([P, PACK], F32, "gm_rows")
        gn_rows = tile([P, PACK], F32, "gn_rows")
        nc.sync.dma_start(out=gm_rows[:], in_=gm.rearrange("(p t) o -> p (t o)", t=PACK))
        nc.sync.dma_start(out=gn_rows[:], in_=gn.rearrange("(p t) o -> p (t o)", t=PACK))
        n6_list = load_list(n6, "n6_list")
        n5_list = load_list(n5, "n5_list")

        y_window = row_tiles(2 * S, "y_window")
        h_window = row_tiles(S, "h_window")
        for window in y_window:
            nc.vector.memset(window[:, S:], 0.0)
        nc.vector.memset(w23_scale_raw[:].bitcast(I32), 0)
        load_scales([nc.sync] * QUADRANTS, w23_scale_raw[:, W3, :], w3_scales)
        load_scales([nc.sync] * QUADRANTS, w23_scale_raw[:, W2, :], w2_scales)

        w1_word_parts = deal_words(w1_word_raw, "w1_word_parts")
        w1_scale_parts = deal_scales(w1_scale_raw, 0, PACK, "w1_scale_parts")
        picked_scales = [tile([P, S // 2], U8, "picked_scales0"), tile([P, S // 2], U8, "picked_scales1", "w1_scale_raw")]
        picked_words = [tile([P, S // 2], U32, "picked_words%d" % j) for j in range(len(halves))]
        for j, cols in enumerate(halves):
            nc.vector.tensor_copy(picked_words[j][:], x_word_table[:].bitcast(U32).indirect(offs_list[:, entries(cols)]))
            nc.vector.tensor_copy(picked_scales[j][:], x_scale_table[:].indirect(offs_list[:, entries(cols)]))
        w23_word_parts = deal_words(w23_word_raw, "w23_word_parts", "x_scale_table")

        st_window = row_tiles(2 * S, "st_window")
        gm_y = tile([P, PACK, S], F32, "gm_y")
        y_banks = []
        for t in range(PACK):
            if t == 0:
                banks = [(psum.tile([P, S // 2], F32, name="y_bank0_%d" % j), cols) for j, cols in enumerate(halves)]
                targets = [bank[:] for bank, cols in banks]
            else:
                banks = [(psum.tile([P, S], F32, name="y_bank%d" % t), slice(0, S))]
                targets = [banks[0][0][:, cols] for cols in halves]
            for j in (0, 1) if t == 0 else (1, 0):
                product(targets[j], w1_word_parts[:, 0, t, :], w1_scale_parts[:, 0, t, :], picked_words[j][:], picked_scales[j][:], True, True)
            y_banks.append(banks)
            copies = [y_window[t][:, :S], st_window[t][:, S:]]
            for copy in copies if t == 0 else reversed(copies):
                for bank, cols in banks:
                    nc.scalar.copy(out=copy[:, cols], in_=bank[:])

        pa = row_tiles(W, "pa")
        minus_pb = row_tiles(W, "minus_pb")
        pa75 = row_tiles(W, "pa75")
        pb75 = row_tiles(W, "pb75")
        dt = row_tiles(S, "dt")
        z2_gate = tile([P, PACK, S], F32, "z2_gate")
        z_woven = tile([P, S, PACK], BF16, "z_woven")
        z2_woven = tile([P, S, PACK], BF16, "z2_woven")

        for t in range(PACK):
            nc.vector.tensor_copy(pa[t][:], y_window[t][:].indirect(n1_list[:]))
            nc.vector.tensor_scalar(minus_pb[t][:], y_window[t][:].indirect(n2_list[:]), -1.0, 0.0, ALU.mult, ALU.add)
            nc.vector.tensor_tensor(st_window[t][:, :S], y_window[t][:].indirect(n3_list[:]), st_window[t][:, S:], ALU.subtract)
            nc.vector.tensor_tensor(dt[t][:].indirect(n2_list[:]), pa[t][:], minus_pb[t][:], ALU.add)
            nc.scalar.activation(out=z2_gate[:, t, :], in_=st_window[t][:].indirect(n4_list[:]), func=ACT.Sigmoid)
            nc.scalar.activation(out=pa75[t][:], in_=pa[t][:], func=ACT.Copy, scale=0.75)
            nc.scalar.activation(out=pb75[t][:], in_=minus_pb[t][:], func=ACT.Copy, scale=-0.75)
            for bank, cols in y_banks[t]:
                nc.scalar.activation(out=gm_y[:, t, cols], in_=bank[:], func=ACT.Copy, scale=gm_rows[:, t : t + 1])
        w23_scale_first = deal_scales(w23_scale_raw, 0, 1, "w23_scale_first", "minus_pb0")
        for t in range(PACK):
            nc.vector.tensor_tensor(dt[t][:].indirect(n1_list[:]), pa75[t][:], pb75[t][:], ALU.add)
            nc.scalar.activation(out=z_woven[:, :, t], in_=dt[t][:], func=ACT.Copy, scale=gn_rows[:, t : t + 1])
        nc.vector.tensor_tensor(
            z2_woven[:].rearrange(WALK_WOVEN, i=2), z2_gate[:].rearrange(WALK_ROW_TILES, i=2),
            gm_y[:].rearrange(WALK_ROW_TILES, i=2), ALU.mult,
        )

        z2_words = tile([P, S], U32, "z2_words")
        z2_scales = tile([P, S], U8, "z2_scales")
        z_words = tile([P, S], U32, "z_words")
        z_scales = tile([P, S], U8, "z_scales")
        quantize(z_words, z_scales, z_woven, halves[0])
        quantize(z2_words, z2_scales, z2_woven, slice(0, S))
        quantize(z_words, z_scales, z_woven, halves[1])

        w23_scale_rest = deal_scales(w23_scale_raw, 1, PACK, "w23_scale_rest", "z_woven")
        free_banks = ("y_bank0_0", "y_bank0_1", "y_bank1", "y_bank2")
        quarter_banks = [psum.tile([P, P], F32, name="h_bank0_%d" % q, tag=tag) for q, tag in enumerate(free_banks)]
        for bank, cols in zip(quarter_banks, quarters):
            product(bank[:], w23_word_parts[:, W3, 0, :], w23_scale_first[:, W3, 0, :], z2_words[:, cols], z2_scales[:, cols], True, False)
        for bank, cols in zip(quarter_banks, quarters):
            product(bank[:], w23_word_parts[:, W2, 0, :], w23_scale_first[:, W2, 0, :], z_words[:, cols], z_scales[:, cols], False, True)
            nc.scalar.copy(out=h_window[0][:, cols], in_=bank[:])
        for t in range(1, PACK):
            bank = psum.tile([P, S], F32, name="h_bank%d" % t)
            product(bank[:], w23_word_parts[:, W3, t, :], w23_scale_rest[:, W3, t - 1, :], z2_words[:], z2_scales[:], True, False)
            product(bank[:], w23_word_parts[:, W2, t, :], w23_scale_rest[:, W2, t - 1, :], z_words[:], z_scales[:], False, True)
            nc.scalar.copy(out=h_window[t][:], in_=bank[:])

        out_rows = out_0.rearrange("(p t) c -> p t c", t=PACK)
        out_word_rows = out_1[0].rearrange("p c r -> p (c r)").bitcast(I32)
        out_scales = tile([P, S], U8, "out_scales")
        out_words = tile([P, S], I32, "out_words")
        out_woven = tile([P, S, PACK], BF16, "out_woven")
        h6 = [tile([P, PACK, S // 2], F32, "h6_%d" % j) for j in range(len(halves))]
        for j, cols in enumerate(halves):
            first_round = j == 0
            difference = tile([P, PACK, S // 2], F32, "difference%d" % j, None if first_round else "h6_0")
            out_gate = tile([P, PACK, S // 2], F32, "out_gate%d" % j)
            result = tile([P, PACK, S // 2], F32, "result%d" % j)

            def apply_gate(t):
                nc.vector.tensor_tensor(result[:, t, :], out_gate[:, t, :], h_window[t][:, cols], ALU.mult)

            for t in range(PACK):
                if first_round:
                    for fetched, half in zip(h6, halves):
                        nc.vector.tensor_copy(fetched[:, t, :], h_window[t][:].indirect(n6_list[:, entries(half)]))
                nc.vector.tensor_tensor(
                    difference[:, t, :], h_window[t][:].indirect(n5_list[:, entries(cols)]), h6[j][:, t, :], ALU.subtract
                )
                nc.scalar.activation(out=out_gate[:, t, :], in_=difference[:, t, :], func=ACT.Sigmoid)
                if t > 0:
                    apply_gate(t - 1)
            apply_gate(PACK - 1)
            nc.sync.dma_start(out=out_rows[:, :, cols], in_=result[:])

            woven_walk = out_woven[:, cols, :].rearrange(WALK_WOVEN, i=2)
            result_walk = result[:].rearrange(WALK_ROW_TILES, i=2)
            if first_round:
                nc.scalar.copy(out=woven_walk, in_=result_walk)
            else:
                pairs_on_scalar = LAST_WEAVE_ON_SCALAR // 2
                nc.scalar.copy(out=woven_walk[:, :pairs_on_scalar], in_=result_walk[:, :pairs_on_scalar])
                nc.vector.tensor_copy(out=woven_walk[:, pairs_on_scalar:], in_=result_walk[:, pairs_on_scalar:])
            quantize(out_words, out_scales, out_woven, cols)
            nc.sync.dma_start(out=out_word_rows[:, cols], in_=out_words[:, cols])
        for q in range(QUADRANTS):
            partitions, rows = scale_rows(q)
            queue = nc.scalar if q % 2 else nc.sync
            queue.dma_start(out=out_2[0, rows, :].bitcast(I32), in_=out_scales[partitions, :].bitcast(I32))
